import numpy as np
import ml_dtypes


def mxq(x, axis, fmt="e4m3"):
    dtype, down = {"e4m3": (ml_dtypes.float8_e4m3fn, 7), "e5m2": (ml_dtypes.float8_e5m2, 14)}[fmt]
    v = np.moveaxis(np.asarray(x, np.float32).astype(ml_dtypes.bfloat16).astype(np.float64), axis, -1)
    blocks = v.reshape(v.shape[:-1] + (-1, 32))
    amax = np.abs(blocks).max(-1, keepdims=True)
    byte = np.maximum(np.where(amax > 0, np.frexp(amax)[1] - 1 + 127, 0) - down, 1)
    scale = np.exp2(byte - 127.0)
    codes = (blocks / scale).astype(np.float32).astype(dtype).astype(np.float64)
    return np.moveaxis((codes * scale).reshape(v.shape), -1, axis)


WIDE = False


def mx_kscale(k):
    if not WIDE:
        return np.ones(k)
    levels = np.array([10, -10, 5, -5, 0])
    if k % 512:
        return np.exp2(np.random.permutation(np.resize(levels, k // 32))).repeat(32)
    a = np.empty((k // 512, 16))
    for p in range(k // 512):
        a[p, :8] = np.random.permutation(np.resize(levels, 8))
        for g in range(8):
            far = levels[np.abs(levels - a[p, g]) >= 10]
            a[p, g + 8] = far[np.random.randint(len(far))]
    return np.exp2(a.ravel()).repeat(32)


BF16 = ml_dtypes.bfloat16


def bf(x):
    return np.asarray(x, np.float32).astype(BF16)


def f64(x):
    return np.asarray(x).astype(np.float64)


E2M1 = np.array([0.0, 0.5, 1.0, 1.5, 2.0, 3.0, 4.0, 6.0, -0.0, -0.5, -1.0, -1.5, -2.0, -3.0, -4.0, -6.0])


def pack_weight(w, fmt):
    k, n = w.shape
    w = f64(bf(w)).reshape(k // 32, 32, n)
    amax = np.abs(w).max(1)
    if fmt == "e4m3":
        byte = np.frexp(amax)[1] - 1 + 127 - 7
    else:
        mant, ex = np.frexp(amax / 6.0)
        byte = np.where(mant > 0.5, ex, ex - 1) + 127
    byte = np.clip(np.where(amax > 0, byte, 1), 1, 254)
    scaled = (w * np.exp2(127.0 - byte)[:, None, :]).reshape(k, n).astype(np.float32)
    by_word = np.ascontiguousarray(scaled.reshape(k // 512, 128, 4, n).transpose(0, 1, 3, 2))
    if fmt == "e4m3":
        words = by_word.astype(ml_dtypes.float8_e4m3fn).view(np.uint8)
    else:
        c = by_word.astype(ml_dtypes.float4_e2m1fn).view(np.uint8) & 0xF
        words = c[..., 0::2] | (c[..., 1::2] << 4)
    return np.ascontiguousarray(words), np.ascontiguousarray(byte.astype(np.uint8).reshape(k // 512, 16, n))


def unpack_weight(words, scales, fmt):
    g, p, n, _ = words.shape
    if fmt == "e4m3":
        vals = np.ascontiguousarray(words).view(ml_dtypes.float8_e4m3fn).astype(np.float64)
    else:
        nib = np.empty((g, p, n, 4), np.uint8)
        nib[..., 0::2] = words & 0xF
        nib[..., 1::2] = words >> 4
        vals = E2M1[nib]
    vals = vals * np.repeat(np.exp2(scales.astype(np.float64) - 127.0), 8, axis=1)[..., None]
    return vals.transpose(0, 1, 3, 2).reshape(g * 512, n)
def pack4(w):
    words, scales = pack_weight(w, "e2m1")
    return words.reshape(words.shape[0], 128, -1), scales


def unpack4(words, scales):
    return unpack_weight(words.reshape(words.shape[0], 128, -1, 2), scales, "e2m1")


M, N, D, R = 1536, 1024, 2048, 512

SPREAD = 0.6
COEF = 1.0


def draw0():
    s = mx_kscale(D)
    t = mx_kscale(M)
    gen = bf(np.random.standard_normal((M, D)) * SPREAD / D ** 0.25 * s)
    real = bf(np.random.standard_normal((N, D)) * SPREAD / D ** 0.25 / s)
    imp = bf((1 + 0.1 * np.random.standard_normal(M)) * t)
    mult_words, mult_scales = pack4(np.random.standard_normal((M, R)) / np.sqrt(M) / t[:, None])
    return {"gen": gen, "real": real, "imp": imp,
            "mult_words": mult_words, "mult_scales": mult_scales}


def core(gen, real, imp, mult_words, mult_scales):
    dots = mxq(f64(gen), 1, "e4m3") @ mxq(f64(real), 1, "e4m3").T
    v = dots + COEF
    ker = v * v * v * f64(imp)[:, None]
    mult = unpack4(mult_words, mult_scales)
    return mult.T @ mxq(ker, 0, "e4m3")


def e4m3fn_bytes(y):
    return np.clip(np.asarray(y, np.float64), -448.0, 448.0).astype(np.float32).astype(ml_dtypes.float8_e4m3fn).view(np.uint8)


def e4m3fn_values(b):
    return np.asarray(b, np.uint8).view(ml_dtypes.float8_e4m3fn).astype(np.float64)


def setup_inputs():
    d = draw0()
    x0 = np.asarray(d['gen']).astype(np.float64)
    s = (np.max(np.abs(x0), axis=(0,), keepdims=True) / 448.0).astype(np.float32)
    out = {}
    for k, v in d.items():
        if k == 'gen':
            out['gen_bytes'] = e4m3fn_bytes(x0 / s.astype(np.float64))
            out['gen_scale'] = s
        else:
            out[k] = v
    return out


def reference(gen_bytes, gen_scale, real, imp, mult_words, mult_scales):
    return core(e4m3fn_values(gen_bytes) * gen_scale.astype(np.float64), real, imp, mult_words, mult_scales)

@@ -1,0 +1,300 @@
+from contextlib import ExitStack
+
+import concourse.mybir as mybir
+from concourse.masks import make_identity
+
+M, N, D, R = 1536, 1024, 2048, 512
+FLOPS = 2 * M * N * D + 2 * M * R * N
+
+F32 = mybir.dt.float32
+BF16 = mybir.dt.bfloat16
+I32 = mybir.dt.int32
+U32 = mybir.dt.uint32
+U8 = mybir.dt.uint8
+FP8 = mybir.dt.float8_e4m3fn
+FP8X4 = mybir.dt.float8_e4m3fn_x4
+FP4X4 = mybir.dt.float4_e2m1fn_x4
+MULT = mybir.AluOpType.mult
+SQUARE = mybir.ActivationFunctionType.Square
+IDENTITY = mybir.ActivationFunctionType.Identity
+
+P = 128
+PACK = 4
+G = D // (P * PACK)
+C = M // (P * PACK)
+H = 2
+HN = N // H
+JT = HN // P
+KT = C * PACK
+B = R // P
+
+
+def tile_kid_bootstrap_witness_s13_kernel(tc, gen_bytes, gen_scale, real, imp, mult_words, mult_scales, out):
+    nc = tc.nc
+    with ExitStack() as ctx:
+        keep = ctx.enter_context(tc.tile_pool(name="keep", bufs=1))
+        work = ctx.enter_context(tc.tile_pool(name="work", bufs=1))
+        psum = ctx.enter_context(tc.psum_pool(name="psum", bufs=8))
+        ctx.enter_context(tc.manual_schedule())
+
+        ident = keep.tile([P, P], F32, name="ident")
+        make_identity(nc, ident[:])
+        scale_row = keep.tile([P, D], F32, name="scale_row")
+        wwords = keep.tile([P, C, 2 * R], U8, name="wwords", align_bytes=64)
+        wscales = keep.tile([P, C, R], U8, name="wscales", align_bytes=64)
+        imp_raw = keep.tile([P, C, PACK], BF16, name="imp_raw")
+        imp32 = keep.tile([P, KT], F32, name="imp32")
+        rcodes = keep.tile([P, G, N], U32, name="rcodes", align_bytes=64)
+        rscales = keep.tile([P, G, N], U8, name="rscales", align_bytes=64)
+
+        nc.gpsimd.memset(wscales[:].rearrange("p c n -> p (c n)").bitcast(I32), 0)
+        nc.gpsimd.dma_start(out=imp_raw[:], in_=imp.rearrange("(c p t) -> p c t", p=P, t=PACK))
+        nc.gpsimd.tensor_copy(out=imp32[:], in_=imp_raw[:].rearrange("p c t -> p (c t)"))
+
+        gen_rows = gen_bytes.rearrange("(c p t) k -> c p t k", p=P, t=PACK)
+        scale_vec = gen_scale.rearrange("o k -> (o k)")
+        gen_tiles = {}
+        real_tiles = {}
+
+        def load_scale(q, n):
+            w = D // n
+            nc.sync.dma_start(out=scale_row[:, q * w : (q + 1) * w], in_=scale_vec[q * w : (q + 1) * w].partition_broadcast(P))
+
+        def load_gen(k):
+            tile = work.tile([P, D], U8, name="codes_in", bufs=8)
+            nc.sync.dma_start(out=tile[:], in_=gen_rows[k // PACK][:, k % PACK, :])
+            gen_tiles[k] = tile
+
+        def load_real(j):
+            tile = work.tile([P, D], BF16, name="real_in", bufs=6)
+            nc.sync.dma_start(out=tile[:], in_=real[j * P : (j + 1) * P, :])
+            real_tiles[j] = tile
+
+        def load_mult():
+            nc.sync.dma_start(out=wwords[:].rearrange("p c n -> p (c n)").bitcast(I32).rearrange("p (c n) -> p c n", c=C),
+                              in_=mult_words.rearrange("c p n -> p c n").bitcast(I32))
+            for q in range(4):
+                nc.sync.dma_start(out=wscales[32 * q : 32 * q + 4].bitcast(I32),
+                                  in_=mult_scales[:, 4 * q : 4 * q + 4, :].rearrange("c q n -> q c n").bitcast(I32))
+
+        wide = {}
+
+        def widen(k, pieces=1, part=None):
+            if k not in wide:
+                made = work.tile([P, D], BF16, name="wide", bufs=6)
+                wide[k] = made
+            tile = wide[k]
+            w = D // pieces
+            for q in part or range(pieces):
+                cols = slice(q * w, (q + 1) * w)
+                nc.vector.tensor_tensor(out=tile[:, cols], in0=gen_tiles[k][:, cols].bitcast(FP8), in1=scale_row[:, cols], op=MULT)
+
+        def turn(src, x):
+            words = src[:].bitcast(F32)
+            bank = psum.tile([P, 512], F32, name="bank")
+            for i in range(2):
+                for u in range(2):
+                    first = 256 * (2 * x + i) + u
+                    col = (2 * i + u) * P
+                    nc.tensor.transpose(bank[:, col : col + P], words[:, first : first + 255 : 2], ident[:])
+            return bank
+
+        def untangle(bank):
+            return bank[:].rearrange("p (g u r) -> p g r u", g=2, u=2)
+
+        turned = {}
+        gen_grouped = {}
+        real_grouped = {}
+
+        def turn_gen(k):
+            turned[k] = [turn(wide[k], x) for x in range(2)]
+
+        def copy_gen(k):
+            tile = work.tile([P, G, P, PACK], BF16, name="gen_grouped", bufs=3, align_bytes=64)
+            w32 = tile[:].rearrange("p g r t -> p (g r t)").bitcast(F32).rearrange("p (g r u) -> p g r u", g=G, u=2)
+            for x in range(2):
+                nc.scalar.copy(out=w32[:, 2 * x : 2 * x + 2], in_=untangle(turned[k][x]))
+            gen_grouped[k] = tile
+
+        def real_tile_steps(j):
+            h = j // JT
+            if h not in real_grouped:
+                grouped = work.tile([P, G, HN, PACK], BF16, name="real_grouped", tag="stage", bufs=4, align_bytes=64)
+                real_grouped[h] = grouped
+            tile = real_grouped[h]
+            w32 = tile[:].rearrange("p g r t -> p (g r t)").bitcast(F32).rearrange("p (g r u) -> p g r u", g=G, u=2)
+            r0 = (j % JT) * P
+            for x in range(2):
+                bank = turn(real_tiles[j], x)
+                nc.scalar.copy(out=w32[:, 2 * x : 2 * x + 2, r0 : r0 + P], in_=untangle(bank))
+
+        gcodes = {}
+
+        def quant_gen(k):
+            codes = work.tile([P, G * P], U32, name="gcodes", bufs=6, align_bytes=64)
+            scales = work.tile([P, G * P], U8, name="gscales", bufs=6, align_bytes=64)
+            nc.vector.quantize_mx(out=codes[:].bitcast(FP8X4), scales=scales[:], in_=gen_grouped[k][:].rearrange("p g r t -> p (g r t)"))
+            gcodes[k] = (codes, scales)
+
+        def quant_real(h, g):
+            cols = slice(h * HN, (h + 1) * HN)
+            nc.vector.quantize_mx(out=rcodes[:, g, cols].bitcast(FP8X4), scales=rscales[:, g, cols],
+                                  in_=real_grouped[h][:, g].rearrange("p r t -> p (r t)"))
+
+        factors = {}
+
+        def dots(k, h):
+            codes, scales = gcodes[k]
+            bank = psum.tile([P, 512], F32, name="bank")
+            cols = slice(h * HN, (h + 1) * HN)
+            for g in range(G):
+                m = slice(g * P, (g + 1) * P)
+                nc.tensor.matmul_mx(out=bank[:], lhsT=codes[:, m].bitcast(FP8X4), lhsT_scale=scales[:, m],
+                                    rhs=rcodes[:, g, cols].bitcast(FP8X4), rhs_scale=rscales[:, g, cols],
+                                    start=(g == 0), stop=(g == G - 1))
+            c, t = k // PACK, k % PACK
+            if t == 0:
+                pair = work.tile([P, 2, PACK, HN], F32, name="factors", tag="stage", bufs=4, align_bytes=64)
+                factors[c, h] = pair
+            pair = factors[c, h]
+            nc.scalar.activation(out=pair[:, 0, t], in_=bank[:], func=SQUARE, bias=1.0)
+            nc.scalar.activation(out=pair[:, 1, t], in_=bank[:], func=IDENTITY, scale=imp32[:, k : k + 1], bias=imp32[:, k : k + 1])
+
+        ker = {}
+        kcodes = {}
+
+        def product(c, h):
+            pair = factors[c, h]
+            tile = work.tile([P, HN, PACK], BF16, name="ker", bufs=2, align_bytes=64)
+            nc.vector.tensor_tensor(out=tile[:].rearrange("p (n i) t -> p n t i", i=4),
+                                    in0=pair[:, 0].rearrange("p t (n i) -> p n t i", i=4),
+                                    in1=pair[:, 1].rearrange("p t (n i) -> p n t i", i=4), op=MULT)
+            ker[c, h] = tile
+
+        def quant_ker(c, h):
+            codes = work.tile([P, HN], U32, name="kcodes", bufs=6, align_bytes=64)
+            scales = work.tile([P, HN], U8, name="kscales", bufs=6, align_bytes=64)
+            nc.vector.quantize_mx(out=codes[:].bitcast(FP8X4), scales=scales[:], in_=ker[c, h][:].rearrange("p n t -> p (n t)"))
+            kcodes[c, h] = (codes, scales)
+
+        sums = {}
+
+        def witness(h, b, chunks):
+            if (h, b) not in sums:
+                bank = psum.tile([P, 512], F32, name="bank")
+                sums[h, b] = bank
+            for c in chunks:
+                codes, scales = kcodes[c, h]
+                nc.tensor.matmul_mx(out=sums[h, b][:], lhsT=wwords[:, c, 2 * P * b : 2 * P * (b + 1)].bitcast(FP4X4),
+                                    lhsT_scale=wscales[:, c, P * b : P * (b + 1)],
+                                    rhs=codes[:].bitcast(FP8X4), rhs_scale=scales[:],
+                                    start=(c == 0), stop=(c == C - 1))
+
+        def emit(h, b, on_vector):
+            tile = work.tile([P, HN], F32, name="result", bufs=4)
+            if on_vector:
+                nc.vector.tensor_copy(out=tile[:], in_=sums[h, b][:])
+            else:
+                nc.scalar.copy(out=tile[:], in_=sums[h, b][:])
+            nc.sync.dma_start(out=out[b * P : (b + 1) * P, h * HN : (h + 1) * HN], in_=tile[:])
+
+        for step in "s0 g0 s1 s2 r0 s3 g1 r1 g2 r2 g3 r3 r4 g4 r5 g5 r6 r7 g6 g7".split():
+            i = int(step[1:])
+            if step[0] == "s":
+                load_scale(i, 4)
+            elif step[0] == "g":
+                load_gen(i)
+            else:
+                load_real(i)
+
+        def gen_tile(k):
+            turn_gen(k)
+            copy_gen(k)
+
+        def quant_reals(h):
+            for g in range(G):
+                quant_real(h, g)
+
+        widen(0, 4, [0, 1])
+        widen(0, 4, [2, 3])
+        real_tile_steps(0)
+        widen(1, 4, [0, 1])
+        widen(1, 4, [2, 3])
+        gen_tile(0)
+        real_tile_steps(1)
+        widen(2)
+        gen_tile(1)
+        real_tile_steps(2)
+        widen(3)
+        quant_gen(0)
+        gen_tile(2)
+        real_tile_steps(3)
+        widen(4)
+        quant_gen(1)
+        gen_tile(3)
+        real_tile_steps(4)
+        quant_reals(0)
+        widen(5)
+        quant_gen(2)
+        real_tile_steps(5)
+        quant_gen(3)
+        real_tile_steps(6)
+        real_tile_steps(7)
+        gen_tile(4)
+        dots(0, 0)
+        dots(1, 0)
+        quant_reals(1)
+        quant_gen(4)
+        gen_tile(5)
+        dots(2, 0)
+        widen(6)
+        dots(3, 0)
+        dots(0, 1)
+        dots(1, 1)
+        for k in range(8):
+            if k + 8 < KT:
+                load_gen(k + 8)
+            if k == 3:
+                load_mult()
+            if k >= 4:
+                dots(k, 0)
+            if k >= 2:
+                dots(k, 1)
+            if k >= 1:
+                quant_gen(k + 4)
+                if k + 5 < KT:
+                    gen_tile(k + 5)
+            if k + 7 < KT:
+                widen(k + 7)
+            if k == 4:
+                product(0, 0)
+            elif k == 5:
+                quant_ker(0, 0)
+            elif k == 6:
+                product(0, 1)
+        quant_ker(0, 1)
+        product(1, 0)
+        for k in range(8, 12):
+            dots(k, 0)
+        quant_ker(1, 0)
+        product(1, 1)
+        dots(8, 1)
+        quant_ker(1, 1)
+        dots(9, 1)
+        product(2, 0)
+        dots(10, 1)
+        quant_ker(2, 0)
+        dots(11, 1)
+        product(2, 1)
+        for b in range(B):
+            witness(0, b, [0, 1])
+        for b in range(B):
+            witness(0, b, [2])
+        for b in range(B):
+            emit(0, b, False)
+        for b in range(B):
+            witness(1, b, [0, 1])
+        quant_ker(2, 1)
+        for b in range(B):
+            witness(1, b, [2])
+            emit(1, b, b % 2 == 1)

@@ -27,6 +27,8 @@ HN = N // H
 JT = HN // P
 KT = C * PACK
 B = R // P
+WARM = 12
+LATE = 4
 
 
 def tile_kid_bootstrap_witness_s13_kernel(tc, gen_bytes, gen_scale, real, imp, mult_words, mult_scales, out):
@@ -40,6 +42,9 @@ def tile_kid_bootstrap_witness_s13_kernel(tc, gen_bytes, gen_scale, real, imp, m
         ident = keep.tile([P, P], F32, name="ident")
         make_identity(nc, ident[:])
         scale_row = keep.tile([P, D], F32, name="scale_row")
+        scale_cols = keep.tile([P, G, PACK], F32, name="scale_cols")
+        warm = keep.tile([P, 512], BF16, name="warm")
+        nc.vector.memset(warm[:], 0.0)
         wwords = keep.tile([P, C, 2 * R], U8, name="wwords", align_bytes=64)
         wscales = keep.tile([P, C, R], U8, name="wscales", align_bytes=64)
         imp_raw = keep.tile([P, C, PACK], BF16, name="imp_raw")
@@ -56,17 +61,19 @@ def tile_kid_bootstrap_witness_s13_kernel(tc, gen_bytes, gen_scale, real, imp, m
         gen_tiles = {}
         real_tiles = {}
 
-        def load_scale(q, n):
-            w = D // n
-            nc.sync.dma_start(out=scale_row[:, q * w : (q + 1) * w], in_=scale_vec[q * w : (q + 1) * w].partition_broadcast(P))
+        nc.scalar.dma_start(out=scale_cols[:], in_=scale_vec.rearrange("(g p t) -> p g t", p=P, t=PACK))
 
-        def load_gen(k):
-            tile = work.tile([P, D], U8, name="codes_in", bufs=8)
-            nc.sync.dma_start(out=tile[:], in_=gen_rows[k // PACK][:, k % PACK, :])
-            gen_tiles[k] = tile
+        def load_scale():
+            nc.sync.dma_start(out=scale_row[:], in_=scale_vec.partition_broadcast(P))
+
+        def load_gen(k, n=2):
+            tile = work.tile([P, n, D], U8, name="codes_in%d" % n, bufs=4 if n == 2 else 2)
+            nc.sync.dma_start(out=tile[:], in_=gen_rows[k // PACK][:, k % PACK : k % PACK + n, :])
+            for i in range(n):
+                gen_tiles[k + i] = tile[:, i, :]
 
         def load_real(j):
-            tile = work.tile([P, D], BF16, name="real_in", bufs=6)
+            tile = work.tile([P, D], BF16, name="real_in", bufs=8)
             nc.sync.dma_start(out=tile[:], in_=real[j * P : (j + 1) * P, :])
             real_tiles[j] = tile
 
@@ -79,15 +86,19 @@ def tile_kid_bootstrap_witness_s13_kernel(tc, gen_bytes, gen_scale, real, imp, m
 
         wide = {}
 
-        def widen(k, pieces=1, part=None):
-            if k not in wide:
-                made = work.tile([P, D], BF16, name="wide", bufs=6)
-                wide[k] = made
-            tile = wide[k]
-            w = D // pieces
-            for q in part or range(pieces):
-                cols = slice(q * w, (q + 1) * w)
-                nc.vector.tensor_tensor(out=tile[:, cols], in0=gen_tiles[k][:, cols].bitcast(FP8), in1=scale_row[:, cols], op=MULT)
+        def widen(k):
+            tile = work.tile([P, D], BF16, name="wide", bufs=6)
+            half = D // 2
+            for q in range(2):
+                cols = slice(q * half, (q + 1) * half)
+                codes = gen_tiles[k][:, cols].bitcast(FP8)
+                if k >= LATE:
+                    nc.vector.tensor_tensor(out=tile[:, cols], in0=codes, in1=scale_row[:, cols], op=MULT)
+                elif k < 2:
+                    nc.vector.tensor_copy(out=tile[:, cols], in_=codes)
+                else:
+                    nc.scalar.copy(out=tile[:, cols], in_=codes)
+            wide[k] = tile
 
         def turn(src, x):
             words = src[:].bitcast(F32)
@@ -113,7 +124,14 @@ def tile_kid_bootstrap_witness_s13_kernel(tc, gen_bytes, gen_scale, real, imp, m
             tile = work.tile([P, G, P, PACK], BF16, name="gen_grouped", bufs=3, align_bytes=64)
             w32 = tile[:].rearrange("p g r t -> p (g r t)").bitcast(F32).rearrange("p (g r u) -> p g r u", g=G, u=2)
             for x in range(2):
-                nc.scalar.copy(out=w32[:, 2 * x : 2 * x + 2], in_=untangle(turned[k][x]))
+                if k >= LATE:
+                    nc.scalar.copy(out=w32[:, 2 * x : 2 * x + 2], in_=untangle(turned[k][x]))
+                    continue
+                values = turned[k][x][:].bitcast(BF16).rearrange("p (g u r e) -> p g r u e", g=2, u=2, e=2)
+                for i in range(2):
+                    g = 2 * x + i
+                    by_k = scale_cols[:, g, :].rearrange("p (u e) -> p u e", u=2).unsqueeze(1).to_broadcast([P, P, 2, 2])
+                    nc.vector.tensor_tensor(out=tile[:, g].rearrange("p r (u e) -> p r u e", u=2), in0=values[:, i], in1=by_k, op=MULT)
             gen_grouped[k] = tile
 
         def real_tile_steps(j):
@@ -198,94 +216,38 @@ def tile_kid_bootstrap_witness_s13_kernel(tc, gen_bytes, gen_scale, real, imp, m
                 nc.scalar.copy(out=tile[:], in_=sums[h, b][:])
             nc.sync.dma_start(out=out[b * P : (b + 1) * P, h * HN : (h + 1) * HN], in_=tile[:])
 
-        for step in "s0 g0 s1 s2 r0 s3 g1 r1 g2 r2 g3 r3 r4 g4 r5 g5 r6 r7 g6 g7".split():
-            i = int(step[1:])
-            if step[0] == "s":
-                load_scale(i, 4)
-            elif step[0] == "g":
-                load_gen(i)
-            else:
-                load_real(i)
-
-        def gen_tile(k):
-            turn_gen(k)
-            copy_gen(k)
+        load_gen(0, 1)
+        load_gen(1, 1)
+        load_gen(2)
+        for j in range(6):
+            load_real(j)
+        load_scale()
+        load_real(6)
+        load_real(7)
+        load_gen(4)
+        load_gen(6)
 
         def quant_reals(h):
             for g in range(G):
                 quant_real(h, g)
 
-        widen(0, 4, [0, 1])
-        widen(0, 4, [2, 3])
-        real_tile_steps(0)
-        widen(1, 4, [0, 1])
-        widen(1, 4, [2, 3])
-        gen_tile(0)
-        real_tile_steps(1)
-        widen(2)
-        gen_tile(1)
-        real_tile_steps(2)
-        widen(3)
-        quant_gen(0)
-        gen_tile(2)
-        real_tile_steps(3)
-        widen(4)
-        quant_gen(1)
-        gen_tile(3)
-        real_tile_steps(4)
-        quant_reals(0)
-        widen(5)
-        quant_gen(2)
-        real_tile_steps(5)
-        quant_gen(3)
-        real_tile_steps(6)
-        real_tile_steps(7)
-        gen_tile(4)
-        dots(0, 0)
-        dots(1, 0)
-        quant_reals(1)
-        quant_gen(4)
-        gen_tile(5)
-        dots(2, 0)
-        widen(6)
-        dots(3, 0)
-        dots(0, 1)
-        dots(1, 1)
-        for k in range(8):
-            if k + 8 < KT:
-                load_gen(k + 8)
-            if k == 3:
+        bank = psum.tile([P, 512], F32, name="bank")
+        for i in range(WARM):
+            nc.tensor.matmul(bank[:], lhsT=warm[:, :P], rhs=warm[:], start=True, stop=True)
+
+        steps = {"W": widen, "T": turn_gen, "C": copy_gen, "R": real_tile_steps, "Q": quant_gen, "H": quant_reals, "L": load_gen}
+        pairs = {"D": dots, "P": product, "K": quant_ker}
+        text = """W0 T0 W2 W1 T1 C0 R0 W3 C1 Q0 T2 R1 C2 Q1 T3 R2 C3 R3 Q2 R4 H0 Q3 W4 R5 R6 R7 D00 D10 W5 D20 T4 C4 D30 H1
+            W6 T5 C5 D01 Q4 L8 W7 D11 T6 C6 W8 D21 Q5 T7 C7 L10 W9 D31 Q6 T8 C8 M W10 D40 D41 Q7 T9 C9 W11 P00 D50 D51 Q8 T10 C10
+            K00 D60 D61 Q9 T11 C11 P01 D70 D71 Q10 K01 P10 Q11 D80 D90 D100 D110 K10 P11 D81 K11 D91 P20 D101 K20 D111 P21"""
+        for step in text.split():
+            if step == "M":
                 load_mult()
-            if k >= 4:
-                dots(k, 0)
-            if k >= 2:
-                dots(k, 1)
-            if k >= 1:
-                quant_gen(k + 4)
-                if k + 5 < KT:
-                    gen_tile(k + 5)
-            if k + 7 < KT:
-                widen(k + 7)
-            if k == 4:
-                product(0, 0)
-            elif k == 5:
-                quant_ker(0, 0)
-            elif k == 6:
-                product(0, 1)
-        quant_ker(0, 1)
-        product(1, 0)
-        for k in range(8, 12):
-            dots(k, 0)
-        quant_ker(1, 0)
-        product(1, 1)
-        dots(8, 1)
-        quant_ker(1, 1)
-        dots(9, 1)
-        product(2, 0)
-        dots(10, 1)
-        quant_ker(2, 0)
-        dots(11, 1)
-        product(2, 1)
+            elif step[0] in steps:
+                steps[step[0]](int(step[1:]))
+            else:
+                pairs[step[0]](int(step[1:-1]), int(step[-1]))
+
         for b in range(B):
             witness(0, b, [0, 1])
         for b in range(B):

@@ -49,8 +49,8 @@ def tile_kid_bootstrap_witness_s13_kernel(tc, gen_bytes, gen_scale, real, imp, m
         wscales = keep.tile([P, C, R], U8, name="wscales", align_bytes=64)
         imp_raw = keep.tile([P, C, PACK], BF16, name="imp_raw")
         imp32 = keep.tile([P, KT], F32, name="imp32")
-        rcodes = keep.tile([P, G, N], U32, name="rcodes", align_bytes=64)
-        rscales = keep.tile([P, G, N], U8, name="rscales", align_bytes=64)
+        rcodes = keep.tile([P, H, G, HN], U32, name="rcodes", align_bytes=64)
+        rscales = keep.tile([P, H, G, HN], U8, name="rscales", align_bytes=64)
 
         nc.gpsimd.memset(wscales[:].rearrange("p c n -> p (c n)").bitcast(I32), 0)
         nc.gpsimd.dma_start(out=imp_raw[:], in_=imp.rearrange("(c p t) -> p c t", p=P, t=PACK))
@@ -85,16 +85,17 @@ def tile_kid_bootstrap_witness_s13_kernel(tc, gen_bytes, gen_scale, real, imp, m
                                   in_=mult_scales[:, 4 * q : 4 * q + 4, :].rearrange("c q n -> q c n").bitcast(I32))
 
         wide = {}
+        counts = {"banks": 0}
 
         def widen(k):
             tile = work.tile([P, D], BF16, name="wide", bufs=6)
+            if k >= LATE:
+                nc.vector.tensor_tensor(out=tile[:], in0=gen_tiles[k].bitcast(FP8), in1=scale_row[:], op=MULT)
             half = D // 2
-            for q in range(2):
+            for q in range(2 if k < LATE else 0):
                 cols = slice(q * half, (q + 1) * half)
                 codes = gen_tiles[k][:, cols].bitcast(FP8)
-                if k >= LATE:
-                    nc.vector.tensor_tensor(out=tile[:, cols], in0=codes, in1=scale_row[:, cols], op=MULT)
-                elif k < 2:
+                if k < 2:
                     nc.vector.tensor_copy(out=tile[:, cols], in_=codes)
                 else:
                     nc.scalar.copy(out=tile[:, cols], in_=codes)
@@ -103,15 +104,18 @@ def tile_kid_bootstrap_witness_s13_kernel(tc, gen_bytes, gen_scale, real, imp, m
         def turn(src, x):
             words = src[:].bitcast(F32)
             bank = psum.tile([P, 512], F32, name="bank")
+            counts["banks"] += 1
+            if counts["banks"] <= 24 and counts["banks"] % 3 == 0:
+                nc.tensor.matmul(bank[:], lhsT=warm[:, :P], rhs=warm[:], start=True, stop=True)
             for i in range(2):
                 for u in range(2):
                     first = 256 * (2 * x + i) + u
-                    col = (2 * i + u) * P
+                    col = (2 * u + i) * P
                     nc.tensor.transpose(bank[:, col : col + P], words[:, first : first + 255 : 2], ident[:])
             return bank
 
         def untangle(bank):
-            return bank[:].rearrange("p (g u r) -> p g r u", g=2, u=2)
+            return bank[:].rearrange("p (u g r) -> p g r u", g=2, u=2)
 
         turned = {}
         gen_grouped = {}
@@ -127,11 +131,10 @@ def tile_kid_bootstrap_witness_s13_kernel(tc, gen_bytes, gen_scale, real, imp, m
                 if k >= LATE:
                     nc.scalar.copy(out=w32[:, 2 * x : 2 * x + 2], in_=untangle(turned[k][x]))
                     continue
-                values = turned[k][x][:].bitcast(BF16).rearrange("p (g u r e) -> p g r u e", g=2, u=2, e=2)
-                for i in range(2):
-                    g = 2 * x + i
-                    by_k = scale_cols[:, g, :].rearrange("p (u e) -> p u e", u=2).unsqueeze(1).to_broadcast([P, P, 2, 2])
-                    nc.vector.tensor_tensor(out=tile[:, g].rearrange("p r (u e) -> p r u e", u=2), in0=values[:, i], in1=by_k, op=MULT)
+                pair = slice(2 * x, 2 * x + 2)
+                values = turned[k][x][:].bitcast(BF16).rearrange("p (u g r e) -> p g r u e", g=2, u=2, e=2)
+                by_k = scale_cols[:, pair].rearrange("p g (u e) -> p g u e", u=2).unsqueeze(2).to_broadcast([P, 2, P, 2, 2])
+                nc.vector.tensor_tensor(out=tile[:, pair].rearrange("p g r (u e) -> p g r u e", u=2), in0=values, in1=by_k, op=MULT)
             gen_grouped[k] = tile
 
         def real_tile_steps(j):
@@ -154,21 +157,22 @@ def tile_kid_bootstrap_witness_s13_kernel(tc, gen_bytes, gen_scale, real, imp, m
             nc.vector.quantize_mx(out=codes[:].bitcast(FP8X4), scales=scales[:], in_=gen_grouped[k][:].rearrange("p g r t -> p (g r t)"))
             gcodes[k] = (codes, scales)
 
-        def quant_real(h, g):
-            cols = slice(h * HN, (h + 1) * HN)
-            nc.vector.quantize_mx(out=rcodes[:, g, cols].bitcast(FP8X4), scales=rscales[:, g, cols],
-                                  in_=real_grouped[h][:, g].rearrange("p r t -> p (r t)"))
+        def quant_reals(h):
+            for x in range(2):
+                pair = slice(2 * x, 2 * x + 2)
+                nc.vector.quantize_mx(out=rcodes[:, h, pair].rearrange("p g n -> p (g n)").bitcast(FP8X4),
+                                      scales=rscales[:, h, pair].rearrange("p g n -> p (g n)"),
+                                      in_=real_grouped[h][:, pair].rearrange("p g r t -> p (g r t)"))
 
         factors = {}
 
         def dots(k, h):
             codes, scales = gcodes[k]
             bank = psum.tile([P, 512], F32, name="bank")
-            cols = slice(h * HN, (h + 1) * HN)
             for g in range(G):
                 m = slice(g * P, (g + 1) * P)
                 nc.tensor.matmul_mx(out=bank[:], lhsT=codes[:, m].bitcast(FP8X4), lhsT_scale=scales[:, m],
-                                    rhs=rcodes[:, g, cols].bitcast(FP8X4), rhs_scale=rscales[:, g, cols],
+                                    rhs=rcodes[:, h, g].bitcast(FP8X4), rhs_scale=rscales[:, h, g],
                                     start=(g == 0), stop=(g == G - 1))
             c, t = k // PACK, k % PACK
             if t == 0:
@@ -226,10 +230,6 @@ def tile_kid_bootstrap_witness_s13_kernel(tc, gen_bytes, gen_scale, real, imp, m
         load_real(7)
         load_gen(4)
         load_gen(6)
-
-        def quant_reals(h):
-            for g in range(G):
-                quant_real(h, g)
 
         bank = psum.tile([P, 512], F32, name="bank")
         for i in range(WARM):

@@ -68,7 +68,9 @@ def tile_kid_bootstrap_witness_s13_kernel(tc, gen_bytes, gen_scale, real, imp, m
 
         def load_gen(k, n=2):
             tile = work.tile([P, n, D], U8, name="codes_in%d" % n, bufs=4 if n == 2 else 2)
-            nc.sync.dma_start(out=tile[:], in_=gen_rows[k // PACK][:, k % PACK : k % PACK + n, :])
+            for q in range(2 if k == 0 else 1):
+                cols = slice(q * D // 2, (q + 1) * D // 2) if k == 0 else slice(0, D)
+                nc.sync.dma_start(out=tile[:, :, cols], in_=gen_rows[k // PACK][:, k % PACK : k % PACK + n, cols])
             for i in range(n):
                 gen_tiles[k + i] = tile[:, i, :]
 
@@ -85,7 +87,6 @@ def tile_kid_bootstrap_witness_s13_kernel(tc, gen_bytes, gen_scale, real, imp, m
                                   in_=mult_scales[:, 4 * q : 4 * q + 4, :].rearrange("c q n -> q c n").bitcast(I32))
 
         wide = {}
-        counts = {"banks": 0}
 
         def widen(k):
             tile = work.tile([P, D], BF16, name="wide", bufs=6)
@@ -95,7 +96,7 @@ def tile_kid_bootstrap_witness_s13_kernel(tc, gen_bytes, gen_scale, real, imp, m
             for q in range(2 if k < LATE else 0):
                 cols = slice(q * half, (q + 1) * half)
                 codes = gen_tiles[k][:, cols].bitcast(FP8)
-                if k < 2:
+                if k < 1:
                     nc.vector.tensor_copy(out=tile[:, cols], in_=codes)
                 else:
                     nc.scalar.copy(out=tile[:, cols], in_=codes)
@@ -104,9 +105,6 @@ def tile_kid_bootstrap_witness_s13_kernel(tc, gen_bytes, gen_scale, real, imp, m
         def turn(src, x):
             words = src[:].bitcast(F32)
             bank = psum.tile([P, 512], F32, name="bank")
-            counts["banks"] += 1
-            if counts["banks"] <= 24 and counts["banks"] % 3 == 0:
-                nc.tensor.matmul(bank[:], lhsT=warm[:, :P], rhs=warm[:], start=True, stop=True)
             for i in range(2):
                 for u in range(2):
                     first = 256 * (2 * x + i) + u
@@ -212,13 +210,16 @@ def tile_kid_bootstrap_witness_s13_kernel(tc, gen_bytes, gen_scale, real, imp, m
                                     rhs=codes[:].bitcast(FP8X4), rhs_scale=scales[:],
                                     start=(c == 0), stop=(c == C - 1))
 
-        def emit(h, b, on_vector):
+        def emit(h, b, on_vector, parts=1):
             tile = work.tile([P, HN], F32, name="result", bufs=4)
-            if on_vector:
-                nc.vector.tensor_copy(out=tile[:], in_=sums[h, b][:])
-            else:
-                nc.scalar.copy(out=tile[:], in_=sums[h, b][:])
-            nc.sync.dma_start(out=out[b * P : (b + 1) * P, h * HN : (h + 1) * HN], in_=tile[:])
+            w = HN // parts
+            for i in range(parts):
+                cols = slice(i * w, (i + 1) * w)
+                if on_vector:
+                    nc.vector.tensor_copy(out=tile[:, cols], in_=sums[h, b][:, cols])
+                else:
+                    nc.scalar.copy(out=tile[:, cols], in_=sums[h, b][:, cols])
+                nc.sync.dma_start(out=out[b * P : (b + 1) * P, h * HN + i * w : h * HN + (i + 1) * w], in_=tile[:, cols])
 
         load_gen(0, 1)
         load_gen(1, 1)
@@ -237,9 +238,9 @@ def tile_kid_bootstrap_witness_s13_kernel(tc, gen_bytes, gen_scale, real, imp, m
 
         steps = {"W": widen, "T": turn_gen, "C": copy_gen, "R": real_tile_steps, "Q": quant_gen, "H": quant_reals, "L": load_gen}
         pairs = {"D": dots, "P": product, "K": quant_ker}
-        text = """W0 T0 W2 W1 T1 C0 R0 W3 C1 Q0 T2 R1 C2 Q1 T3 R2 C3 R3 Q2 R4 H0 Q3 W4 R5 R6 R7 D00 D10 W5 D20 T4 C4 D30 H1
-            W6 T5 C5 D01 Q4 L8 W7 D11 T6 C6 W8 D21 Q5 T7 C7 L10 W9 D31 Q6 T8 C8 M W10 D40 D41 Q7 T9 C9 W11 P00 D50 D51 Q8 T10 C10
-            K00 D60 D61 Q9 T11 C11 P01 D70 D71 Q10 K01 P10 Q11 D80 D90 D100 D110 K10 P11 D81 K11 D91 P20 D101 K20 D111 P21"""
+        text = """W0 T0 W1 T1 W2 C0 R0 W3 C1 Q0 T2 R1 C2 Q1 T3 R2 C3 R3 Q2 R4 H0 Q3 W4 R5 R6 R7 D00 D10 W5 D20 T4 C4 D30 H1
+            W6 T5 C5 D01 Q4 L8 W7 D11 T6 C6 W8 D21 Q5 T7 C7 L10 W9 D31 Q6 T8 C8 M W10 D40 D41 Q7 T9 C9 W11 D50 D51 Q8 T10 C10
+            P00 Q9 T11 C11 D60 D61 K00 Q10 P01 Q11 D70 D71 K01 P10 D80 D90 D100 D110 K10 P11 D81 K11 D91 P20 D101 K20 D111 P21"""
         for step in text.split():
             if step == "M":
                 load_mult()
@@ -259,4 +260,4 @@ def tile_kid_bootstrap_witness_s13_kernel(tc, gen_bytes, gen_scale, real, imp, m
         quant_ker(2, 1)
         for b in range(B):
             witness(1, b, [2])
-            emit(1, b, b % 2 == 1)
+            emit(1, b, b % 2 == 1, 1 if b < 2 else 2)

@@ -28,7 +28,7 @@ JT = HN // P
 KT = C * PACK
 B = R // P
 WARM = 12
-LATE = 4
+LATE = 5
 
 
 def tile_kid_bootstrap_witness_s13_kernel(tc, gen_bytes, gen_scale, real, imp, mult_words, mult_scales, out):
@@ -224,12 +224,10 @@ def tile_kid_bootstrap_witness_s13_kernel(tc, gen_bytes, gen_scale, real, imp, m
         load_gen(0, 1)
         load_gen(1, 1)
         load_gen(2)
-        for j in range(6):
+        for j in range(H * JT):
             load_real(j)
-        load_scale()
-        load_real(6)
-        load_real(7)
         load_gen(4)
+        load_scale()
         load_gen(6)
 
         bank = psum.tile([P, 512], F32, name="bank")
@@ -238,8 +236,8 @@ def tile_kid_bootstrap_witness_s13_kernel(tc, gen_bytes, gen_scale, real, imp, m
 
         steps = {"W": widen, "T": turn_gen, "C": copy_gen, "R": real_tile_steps, "Q": quant_gen, "H": quant_reals, "L": load_gen}
         pairs = {"D": dots, "P": product, "K": quant_ker}
-        text = """W0 T0 W1 T1 W2 C0 R0 W3 C1 Q0 T2 R1 C2 Q1 T3 R2 C3 R3 Q2 R4 H0 Q3 W4 R5 R6 R7 D00 D10 W5 D20 T4 C4 D30 H1
-            W6 T5 C5 D01 Q4 L8 W7 D11 T6 C6 W8 D21 Q5 T7 C7 L10 W9 D31 Q6 T8 C8 M W10 D40 D41 Q7 T9 C9 W11 D50 D51 Q8 T10 C10
+        text = """W0 T0 W1 T1 W2 C0 R0 W3 C1 Q0 T2 R1 C2 Q1 R2 Q2 T3 R3 C3 R4 H0 W4 R5 Q3 R6 T4 C4 R7 D00 D10 W5 H1 D20 Q4 D30 T5 C5
+            W6 D01 Q5 D11 L8 W7 T6 C6 D21 W8 D31 T7 C7 L10 W9 Q6 T8 C8 M W10 D40 D41 Q7 T9 C9 W11 D50 D51 Q8 T10 C10
             P00 Q9 T11 C11 D60 D61 K00 Q10 P01 Q11 D70 D71 K01 P10 D80 D90 D100 D110 K10 P11 D81 K11 D91 P20 D101 K20 D111 P21"""
         for step in text.split():
             if step == "M":

from contextlib import ExitStack

import concourse.mybir as mybir
from concourse.masks import make_identity

M, N, D, R = 1536, 1024, 2048, 512
FLOPS = 2 * M * N * D + 2 * M * R * N

F32 = mybir.dt.float32
BF16 = mybir.dt.bfloat16
I32 = mybir.dt.int32
U32 = mybir.dt.uint32
U8 = mybir.dt.uint8
FP8 = mybir.dt.float8_e4m3fn
FP8X4 = mybir.dt.float8_e4m3fn_x4
FP4X4 = mybir.dt.float4_e2m1fn_x4
MULT = mybir.AluOpType.mult
SQUARE = mybir.ActivationFunctionType.Square
IDENTITY = mybir.ActivationFunctionType.Identity

P = 128
PACK = 4
G = D // (P * PACK)
C = M // (P * PACK)
H = 2
HN = N // H
JT = HN // P
KT = C * PACK
B = R // P
WARM = 12
LATE = 5


def tile_kid_bootstrap_witness_s13_kernel(tc, gen_bytes, gen_scale, real, imp, mult_words, mult_scales, out):
    nc = tc.nc
    with ExitStack() as ctx:
        keep = ctx.enter_context(tc.tile_pool(name="keep", bufs=1))
        work = ctx.enter_context(tc.tile_pool(name="work", bufs=1))
        psum = ctx.enter_context(tc.psum_pool(name="psum", bufs=8))
        ctx.enter_context(tc.manual_schedule())

        ident = keep.tile([P, P], F32, name="ident")
        make_identity(nc, ident[:])
        scale_row = keep.tile([P, D], F32, name="scale_row")
        scale_cols = keep.tile([P, G, PACK], F32, name="scale_cols")
        warm = keep.tile([P, 512], BF16, name="warm")
        nc.vector.memset(warm[:], 0.0)
        wwords = keep.tile([P, C, 2 * R], U8, name="wwords", align_bytes=64)
        wscales = keep.tile([P, C, R], U8, name="wscales", align_bytes=64)
        imp_raw = keep.tile([P, C, PACK], BF16, name="imp_raw")
        imp32 = keep.tile([P, KT], F32, name="imp32")
        rcodes = keep.tile([P, H, G, HN], U32, name="rcodes", align_bytes=64)
        rscales = keep.tile([P, H, G, HN], U8, name="rscales", align_bytes=64)

        nc.gpsimd.memset(wscales[:].rearrange("p c n -> p (c n)").bitcast(I32), 0)
        nc.gpsimd.dma_start(out=imp_raw[:], in_=imp.rearrange("(c p t) -> p c t", p=P, t=PACK))
        nc.gpsimd.tensor_copy(out=imp32[:], in_=imp_raw[:].rearrange("p c t -> p (c t)"))

        gen_rows = gen_bytes.rearrange("(c p t) k -> c p t k", p=P, t=PACK)
        scale_vec = gen_scale.rearrange("o k -> (o k)")
        gen_tiles = {}
        real_tiles = {}

        nc.scalar.dma_start(out=scale_cols[:], in_=scale_vec.rearrange("(g p t) -> p g t", p=P, t=PACK))

        def load_scale():
            nc.sync.dma_start(out=scale_row[:], in_=scale_vec.partition_broadcast(P))

        def load_gen(k, n=2):
            tile = work.tile([P, n, D], U8, name="codes_in%d" % n, bufs=4 if n == 2 else 2)
            for q in range(2 if k == 0 else 1):
                cols = slice(q * D // 2, (q + 1) * D // 2) if k == 0 else slice(0, D)
                nc.sync.dma_start(out=tile[:, :, cols], in_=gen_rows[k // PACK][:, k % PACK : k % PACK + n, cols])
            for i in range(n):
                gen_tiles[k + i] = tile[:, i, :]

        def load_real(j):
            tile = work.tile([P, D], BF16, name="real_in", bufs=8)
            nc.sync.dma_start(out=tile[:], in_=real[j * P : (j + 1) * P, :])
            real_tiles[j] = tile

        def load_mult():
            nc.sync.dma_start(out=wwords[:].rearrange("p c n -> p (c n)").bitcast(I32).rearrange("p (c n) -> p c n", c=C),
                              in_=mult_words.rearrange("c p n -> p c n").bitcast(I32))
            for q in range(4):
                nc.sync.dma_start(out=wscales[32 * q : 32 * q + 4].bitcast(I32),
                                  in_=mult_scales[:, 4 * q : 4 * q + 4, :].rearrange("c q n -> q c n").bitcast(I32))

        wide = {}

        def widen(k):
            tile = work.tile([P, D], BF16, name="wide", bufs=6)
            if k >= LATE:
                nc.vector.tensor_tensor(out=tile[:], in0=gen_tiles[k].bitcast(FP8), in1=scale_row[:], op=MULT)
            half = D // 2
            for q in range(2 if k < LATE else 0):
                cols = slice(q * half, (q + 1) * half)
                codes = gen_tiles[k][:, cols].bitcast(FP8)
                if k < 1:
                    nc.vector.tensor_copy(out=tile[:, cols], in_=codes)
                else:
                    nc.scalar.copy(out=tile[:, cols], in_=codes)
            wide[k] = tile

        def turn(src, x):
            words = src[:].bitcast(F32)
            bank = psum.tile([P, 512], F32, name="bank")
            for i in range(2):
                for u in range(2):
                    first = 256 * (2 * x + i) + u
                    col = (2 * u + i) * P
                    nc.tensor.transpose(bank[:, col : col + P], words[:, first : first + 255 : 2], ident[:])
            return bank

        def untangle(bank):
            return bank[:].rearrange("p (u g r) -> p g r u", g=2, u=2)

        turned = {}
        gen_grouped = {}
        real_grouped = {}

        def turn_gen(k):
            turned[k] = [turn(wide[k], x) for x in range(2)]

        def copy_gen(k):
            tile = work.tile([P, G, P, PACK], BF16, name="gen_grouped", bufs=3, align_bytes=64)
            w32 = tile[:].rearrange("p g r t -> p (g r t)").bitcast(F32).rearrange("p (g r u) -> p g r u", g=G, u=2)
            for x in range(2):
                if k >= LATE:
                    nc.scalar.copy(out=w32[:, 2 * x : 2 * x + 2], in_=untangle(turned[k][x]))
                    continue
                pair = slice(2 * x, 2 * x + 2)
                values = turned[k][x][:].bitcast(BF16).rearrange("p (u g r e) -> p g r u e", g=2, u=2, e=2)
                by_k = scale_cols[:, pair].rearrange("p g (u e) -> p g u e", u=2).unsqueeze(2).to_broadcast([P, 2, P, 2, 2])
                nc.vector.tensor_tensor(out=tile[:, pair].rearrange("p g r (u e) -> p g r u e", u=2), in0=values, in1=by_k, op=MULT)
            gen_grouped[k] = tile

        def real_tile_steps(j):
            h = j // JT
            if h not in real_grouped:
                grouped = work.tile([P, G, HN, PACK], BF16, name="real_grouped", tag="stage", bufs=4, align_bytes=64)
                real_grouped[h] = grouped
            tile = real_grouped[h]
            w32 = tile[:].rearrange("p g r t -> p (g r t)").bitcast(F32).rearrange("p (g r u) -> p g r u", g=G, u=2)
            r0 = (j % JT) * P
            for x in range(2):
                bank = turn(real_tiles[j], x)
                nc.scalar.copy(out=w32[:, 2 * x : 2 * x + 2, r0 : r0 + P], in_=untangle(bank))

        gcodes = {}

        def quant_gen(k):
            codes = work.tile([P, G * P], U32, name="gcodes", bufs=6, align_bytes=64)
            scales = work.tile([P, G * P], U8, name="gscales", bufs=6, align_bytes=64)
            nc.vector.quantize_mx(out=codes[:].bitcast(FP8X4), scales=scales[:], in_=gen_grouped[k][:].rearrange("p g r t -> p (g r t)"))
            gcodes[k] = (codes, scales)

        def quant_reals(h):
            for x in range(2):
                pair = slice(2 * x, 2 * x + 2)
                nc.vector.quantize_mx(out=rcodes[:, h, pair].rearrange("p g n -> p (g n)").bitcast(FP8X4),
                                      scales=rscales[:, h, pair].rearrange("p g n -> p (g n)"),
                                      in_=real_grouped[h][:, pair].rearrange("p g r t -> p (g r t)"))

        factors = {}

        def dots(k, h):
            codes, scales = gcodes[k]
            bank = psum.tile([P, 512], F32, name="bank")
            for g in range(G):
                m = slice(g * P, (g + 1) * P)
                nc.tensor.matmul_mx(out=bank[:], lhsT=codes[:, m].bitcast(FP8X4), lhsT_scale=scales[:, m],
                                    rhs=rcodes[:, h, g].bitcast(FP8X4), rhs_scale=rscales[:, h, g],
                                    start=(g == 0), stop=(g == G - 1))
            c, t = k // PACK, k % PACK
            if t == 0:
                pair = work.tile([P, 2, PACK, HN], F32, name="factors", tag="stage", bufs=4, align_bytes=64)
                factors[c, h] = pair
            pair = factors[c, h]
            nc.scalar.activation(out=pair[:, 0, t], in_=bank[:], func=SQUARE, bias=1.0)
            nc.scalar.activation(out=pair[:, 1, t], in_=bank[:], func=IDENTITY, scale=imp32[:, k : k + 1], bias=imp32[:, k : k + 1])

        ker = {}
        kcodes = {}

        def product(c, h):
            pair = factors[c, h]
            tile = work.tile([P, HN, PACK], BF16, name="ker", bufs=2, align_bytes=64)
            nc.vector.tensor_tensor(out=tile[:].rearrange("p (n i) t -> p n t i", i=4),
                                    in0=pair[:, 0].rearrange("p t (n i) -> p n t i", i=4),
                                    in1=pair[:, 1].rearrange("p t (n i) -> p n t i", i=4), op=MULT)
            ker[c, h] = tile

        def quant_ker(c, h):
            codes = work.tile([P, HN], U32, name="kcodes", bufs=6, align_bytes=64)
            scales = work.tile([P, HN], U8, name="kscales", bufs=6, align_bytes=64)
            nc.vector.quantize_mx(out=codes[:].bitcast(FP8X4), scales=scales[:], in_=ker[c, h][:].rearrange("p n t -> p (n t)"))
            kcodes[c, h] = (codes, scales)

        sums = {}

        def witness(h, b, chunks):
            if (h, b) not in sums:
                bank = psum.tile([P, 512], F32, name="bank")
                sums[h, b] = bank
            for c in chunks:
                codes, scales = kcodes[c, h]
                nc.tensor.matmul_mx(out=sums[h, b][:], lhsT=wwords[:, c, 2 * P * b : 2 * P * (b + 1)].bitcast(FP4X4),
                                    lhsT_scale=wscales[:, c, P * b : P * (b + 1)],
                                    rhs=codes[:].bitcast(FP8X4), rhs_scale=scales[:],
                                    start=(c == 0), stop=(c == C - 1))

        def emit(h, b, on_vector, parts=1):
            tile = work.tile([P, HN], F32, name="result", bufs=4)
            w = HN // parts
            for i in range(parts):
                cols = slice(i * w, (i + 1) * w)
                if on_vector:
                    nc.vector.tensor_copy(out=tile[:, cols], in_=sums[h, b][:, cols])
                else:
                    nc.scalar.copy(out=tile[:, cols], in_=sums[h, b][:, cols])
                nc.sync.dma_start(out=out[b * P : (b + 1) * P, h * HN + i * w : h * HN + (i + 1) * w], in_=tile[:, cols])

        load_gen(0, 1)
        load_gen(1, 1)
        load_gen(2)
        for j in range(H * JT):
            load_real(j)
        load_gen(4)
        load_scale()
        load_gen(6)

        bank = psum.tile([P, 512], F32, name="bank")
        for i in range(WARM):
            nc.tensor.matmul(bank[:], lhsT=warm[:, :P], rhs=warm[:], start=True, stop=True)

        steps = {"W": widen, "T": turn_gen, "C": copy_gen, "R": real_tile_steps, "Q": quant_gen, "H": quant_reals, "L": load_gen}
        pairs = {"D": dots, "P": product, "K": quant_ker}
        text = """W0 T0 W1 T1 W2 C0 R0 W3 C1 Q0 T2 R1 C2 Q1 R2 Q2 T3 R3 C3 R4 H0 W4 R5 Q3 R6 T4 C4 R7 D00 D10 W5 H1 D20 Q4 D30 T5 C5
            W6 D01 Q5 D11 L8 W7 T6 C6 D21 W8 D31 T7 C7 L10 W9 Q6 T8 C8 M W10 D40 D41 Q7 T9 C9 W11 D50 D51 Q8 T10 C10
            P00 Q9 T11 C11 D60 D61 K00 Q10 P01 Q11 D70 D71 K01 P10 D80 D90 D100 D110 K10 P11 D81 K11 D91 P20 D101 K20 D111 P21"""
        for step in text.split():
            if step == "M":
                load_mult()
            elif step[0] in steps:
                steps[step[0]](int(step[1:]))
            else:
                pairs[step[0]](int(step[1:-1]), int(step[-1]))

        for b in range(B):
            witness(0, b, [0, 1])
        for b in range(B):
            witness(0, b, [2])
        for b in range(B):
            emit(0, b, False)
        for b in range(B):
            witness(1, b, [0, 1])
        quant_ker(2, 1)
        for b in range(B):
            witness(1, b, [2])
            emit(1, b, b % 2 == 1, 1 if b < 2 else 2)
